import numpy as np
import ml_dtypes


def mxq(x, axis, fmt="e4m3"):
    dtype, down = {"e4m3": (ml_dtypes.float8_e4m3fn, 7), "e5m2": (ml_dtypes.float8_e5m2, 14)}[fmt]
    v = np.moveaxis(np.asarray(x, np.float32).astype(ml_dtypes.bfloat16).astype(np.float64), axis, -1)
    blocks = v.reshape(v.shape[:-1] + (-1, 32))
    amax = np.abs(blocks).max(-1, keepdims=True)
    byte = np.maximum(np.where(amax > 0, np.frexp(amax)[1] - 1 + 127, 0) - down, 1)
    scale = np.exp2(byte - 127.0)
    codes = (blocks / scale).astype(np.float32).astype(dtype).astype(np.float64)
    return np.moveaxis((codes * scale).reshape(v.shape), -1, axis)


WIDE = False


def mx_kscale(k):
    if not WIDE:
        return np.ones(k)
    levels = np.array([30, -30])
    if k % 512:
        return np.exp2(np.random.permutation(np.resize(levels, k // 32))).repeat(32)
    a = np.empty((k // 512, 16))
    for p in range(k // 512):
        a[p, :8] = np.random.permutation(np.resize(levels, 8))
        for g in range(8):
            far = levels[np.abs(levels - a[p, g]) >= 10]
            a[p, g + 8] = far[np.random.randint(len(far))]
    return np.exp2(a.ravel()).repeat(32)


def f64(x):
    return np.asarray(x).astype(np.float64)


E2M1 = np.array([0.0, 0.5, 1.0, 1.5, 2.0, 3.0, 4.0, 6.0, -0.0, -0.5, -1.0, -1.5, -2.0, -3.0, -4.0, -6.0])


def pack_weight(w, fmt):
    k, n = w.shape
    w = f64(np.asarray(w, np.float32).astype(ml_dtypes.bfloat16)).reshape(k // 32, 32, n)
    amax = np.abs(w).max(1)
    if fmt == "e4m3":
        byte = np.frexp(amax)[1] - 1 + 127 - 7
    else:
        mant, ex = np.frexp(amax / 6.0)
        byte = np.where(mant > 0.5, ex, ex - 1) + 127
    byte = np.clip(np.where(amax > 0, byte, 1), 1, 254)
    scaled = (w * np.exp2(127.0 - byte)[:, None, :]).reshape(k, n).astype(np.float32)
    by_word = np.ascontiguousarray(scaled.reshape(k // 512, 128, 4, n).transpose(0, 1, 3, 2))
    if fmt == "e4m3":
        words = by_word.astype(ml_dtypes.float8_e4m3fn).view(np.uint8)
    else:
        c = by_word.astype(ml_dtypes.float4_e2m1fn).view(np.uint8) & 0xF
        words = (c[..., 0::2] | (c[..., 1::2] << 4)).reshape(k // 512, 128, 2 * n)
    return np.ascontiguousarray(words), np.ascontiguousarray(byte.astype(np.uint8).reshape(k // 512, 16, n))


def unpack_weight(words, scales, fmt):
    g, _, n = scales.shape
    words = np.ascontiguousarray(words).reshape(g, 128, n, -1)
    if fmt == "e4m3":
        vals = words.view(ml_dtypes.float8_e4m3fn).astype(np.float64)
    else:
        nib = np.empty((g, 128, n, 4), np.uint8)
        nib[..., 0::2] = words & 0xF
        nib[..., 1::2] = words >> 4
        vals = E2M1[nib]
    vals = vals * np.repeat(np.exp2(scales.astype(np.float64) - 127.0), 8, axis=1)[..., None]
    return vals.transpose(0, 1, 3, 2).reshape(g * 512, n)


K, L, R, M, T = 1536, 1536, 1024, 512, 512


def setup_inputs():
    n = np.random.standard_normal
    s1 = mx_kscale(K)[:, None]
    s2 = mx_kscale(L)[:, None]
    u = mx_kscale(R)[:, None]
    p_w = pack_weight(n((R, M)) / np.sqrt(R) / u, "e2m1")
    return {
        "x": (n((K, T)) * s1).astype(np.float32),
        "wx": (n((K, R)) / np.sqrt(K) / s1 * u.T).astype(np.float32),
        "c": (n((L, T)) * s2).astype(np.float32),
        "wc": (n((L, R)) / np.sqrt(L) / s2).astype(np.float32),
        "w_words": p_w[0],
        "w_scales": p_w[1],
    }


def reference(x, wx, c, wc, w_words, w_scales):
    x_ = mxq(f64(x), 0, "e4m3")
    wx_ = mxq(f64(wx), 0, "e4m3")
    c_ = mxq(f64(c), 0, "e5m2")
    wc_ = mxq(f64(wc), 0, "e4m3")
    w_ = unpack_weight(w_words, w_scales, "e2m1")
    h_ = mxq((wx_.T @ x_) * (wc_.T @ c_), 0, "e4m3")
    y = h_.T @ w_
    return y

@@ -1,0 +1,287 @@
+from contextlib import ExitStack
+
+import concourse.mybir as mybir
+
+K, L, R, M, T = 1536, 1536, 1024, 512, 512
+FLOPS = 2 * (K * R * T + L * R * T + R * M * T)
+
+F32 = mybir.dt.float32
+BF16 = mybir.dt.bfloat16
+U32 = mybir.dt.uint32
+I32 = mybir.dt.int32
+U8 = mybir.dt.uint8
+E4M3 = mybir.dt.float8_e4m3fn_x4
+E5M2 = mybir.dt.float8_e5m2_x4
+E2M1 = mybir.dt.float4_e2m1fn_x4
+
+P = 128
+PACK = 4
+K_PASS = P * PACK
+PASSES = K // K_PASS
+GROUPS = R // K_PASS
+CHUNK = 128
+CHUNKS = T // CHUNK
+UNIT = 256
+
+
+def tile_mix_bilin_tm_none_kernel(tc, x, wx, c, wc, w_words, w_scales, out):
+    nc = tc.nc
+
+    with ExitStack() as ctx:
+        raw = ctx.enter_context(tc.tile_pool(name="raw", bufs=1))
+        stage = ctx.enter_context(tc.tile_pool(name="stage", bufs=8))
+        keep = ctx.enter_context(tc.tile_pool(name="keep", bufs=1))
+        psum = ctx.enter_context(tc.psum_pool(name="psum", bufs=1))
+        ctx.enter_context(tc.manual_schedule())
+
+        def load(src, g, col0, width, tag, bufs):
+            tile = raw.tile([P, PACK, width], F32, name=tag, tag=tag, bufs=bufs)
+            rows = src[g * K_PASS : (g + 1) * K_PASS, col0 : col0 + width]
+            nc.sync.dma_start(out=tile[:], in_=rows.rearrange("(p j) w -> p j w", j=PACK))
+            return tile
+
+        def copy(engine, dst, src):
+            if engine == "vector":
+                nc.vector.tensor_copy(out=dst, in_=src)
+            else:
+                nc.scalar.copy(out=dst, in_=src)
+
+        def round_stream(engine, tile, col0, width):
+            rounded = stage.tile([P, PACK * width], BF16, name="rounded", tag="rounded", align_bytes=64)
+            copy(
+                engine,
+                rounded[:].rearrange("p (c i j) -> p c j i", i=2, j=PACK),
+                tile[:, :, col0 : col0 + width].rearrange("p j (c i) -> p c j i", i=2),
+            )
+            return rounded
+
+        def round_weight(engine, tile, col0, u, width=K_PASS):
+            rounded = stage.tile([P, 2 * width], BF16, name="rounded", tag="rounded", align_bytes=64)
+            src = tile[:, :, col0 : col0 + width].rearrange("p j (m u i) -> p u m j i", u=2, i=2)
+            copy(engine, rounded[:].rearrange("p (i m j) -> p m j i", i=2, j=PACK), src[:, u])
+            return rounded
+
+        def operand(name, width):
+            codes = keep.tile([P, width], U32, name=name + "_codes", align_bytes=64)
+            scales = keep.tile([P, width], U8, name=name + "_scales", align_bytes=64)
+            return codes, scales
+
+        def quantize(dst, col0, rounded, fmt):
+            width = rounded.shape[1] // PACK
+            nc.vector.quantize_mx(
+                out=dst[0][:, col0 : col0 + width].bitcast(fmt),
+                scales=dst[1][:, col0 : col0 + width],
+                in_=rounded,
+            )
+
+        def bank(b):
+            return psum.tile([P, 512], F32, name="bank%d" % b, tag="bank%d" % b)
+
+        c_raw = [load(c, 0, 0, T, "wide", 6)]
+        wc_raw = [load(wc, 0, 0, R, "wc", PASSES)]
+        w_plane = keep.tile([P, GROUPS, M], U8, name="w_plane", align_bytes=64)
+        nc.vector.memset(w_plane[:].bitcast(I32), 0)
+        for q in range(4):
+            nc.scalar.dma_start(
+                out=w_plane[32 * q : 32 * q + 4].bitcast(I32),
+                in_=w_scales[:, 4 * q : 4 * q + 4, :].rearrange("a r n -> r a n").bitcast(I32),
+            )
+        for g in range(1, PASSES):
+            c_raw.append(load(c, g, 0, T, "wide", 6))
+            wc_raw.append(load(wc, g, 0, R, "wc", PASSES))
+        x01_raw = [load(x, g, 0, 2 * CHUNK, "x01", PASSES) for g in range(PASSES)]
+        wx_raw = {}
+        for g in range(PASSES):
+            wx_raw[0, g] = load(wx, g, 0, K_PASS, "wide", 6)
+
+        pc_banks = [bank(b) for b in range(GROUPS * PACK)]
+        for g in range(PASSES):
+            c_q = operand("c%d" % g, T)
+            first = round_stream("scalar", c_raw[g], 0, UNIT)
+            second = round_stream("vector", c_raw[g], UNIT, UNIT)
+            quantize(c_q, UNIT, second, E5M2)
+            quantize(c_q, 0, first, E5M2)
+            rounded = {}
+            for a in range(GROUPS):
+                rounded[a, 0] = round_weight("scalar", wc_raw[g], a * K_PASS, 0)
+                rounded[a, 1] = round_weight("vector", wc_raw[g], a * K_PASS, 1)
+            for a in range(GROUPS):
+                for u in (1, 0):
+                    wc_q = operand("wc%d%d%d" % (g, a, u), UNIT)
+                    quantize(wc_q, 0, rounded[a, u], E4M3)
+                    for i in range(2):
+                        cols = slice(i * P, (i + 1) * P)
+                        nc.tensor.matmul_mx(
+                            out=pc_banks[a * PACK + 2 * u + i][:],
+                            lhsT=wc_q[0][:, cols].bitcast(E4M3),
+                            lhsT_scale=wc_q[1][:, cols],
+                            rhs=c_q[0][:].bitcast(E5M2),
+                            rhs_scale=c_q[1][:],
+                            start=(g == 0),
+                            stop=(g == PASSES - 1),
+                        )
+
+        for g in range(PASSES - 1):
+            wx_raw[1, g] = load(wx, g, K_PASS, K_PASS, "wide", 6)
+        wx_last = [load(wx, PASSES - 1, K_PASS + n * UNIT, UNIT, "wx_last", 2) for n in range(2)]
+        x2_raw = [load(x, g, 2 * CHUNK, CHUNK, "x2", PASSES) for g in range(PASSES)]
+        w_codes = keep.tile([P, GROUPS, 2 * M], U8, name="w_codes", align_bytes=64)
+        nc.sync.dma_start(out=w_codes[:].bitcast(I32), in_=w_words.rearrange("a p n -> p a n").bitcast(I32))
+        x3_raw = [load(x, g, 3 * CHUNK, CHUNK, "x3", PASSES) for g in range(PASSES)]
+
+        pc = [keep.tile([P, PACK, T], F32, name="pc%d" % a) for a in range(GROUPS)]
+
+        def save_pc(a):
+            for j in (2, 3, 0, 1):
+                nc.scalar.copy(out=pc[a][:, j, :], in_=pc_banks[a * PACK + j][:])
+
+        wx_q, x_q, px, h_rounded, h_q, y = {}, {}, {}, {}, {}, {}
+
+        def prepare_wx(a, g, engines):
+            rounded = [round_weight(engines[u], wx_raw[a, g], 0, u) for u in range(2)]
+            for u in (1, 0):
+                wx_q[a, g, u] = operand("wx%d%d%d" % (a, g, u), UNIT)
+                quantize(wx_q[a, g, u], 0, rounded[u], E4M3)
+
+        def quantize_x(g, t, rounded):
+            chunks = rounded.shape[1] // (PACK * CHUNK)
+            dst = operand("x%d%d" % (g, t), chunks * CHUNK)
+            quantize(dst, 0, rounded, E4M3)
+            for n in range(chunks):
+                cols = slice(n * CHUNK, (n + 1) * CHUNK)
+                x_q[g, t + n] = (dst[0][:, cols], dst[1][:, cols])
+
+        def px_pass(a, t, g):
+            if g == 0:
+                px[a, t] = bank(2 * (t // 2) * 2 + (2 * a + t if t < 2 else 2 * (t - 2) + a))
+            for n, j in enumerate((2, 3, 0, 1)):
+                codes, scales = wx_q[a, g, j // 2]
+                cols = slice((j % 2) * P, (j % 2 + 1) * P)
+                nc.tensor.matmul_mx(
+                    out=px[a, t][:, j * CHUNK : (j + 1) * CHUNK],
+                    lhsT=codes[:, cols].bitcast(E4M3),
+                    lhsT_scale=scales[:, cols],
+                    rhs=x_q[g, t][0].bitcast(E4M3),
+                    rhs_scale=x_q[g, t][1],
+                    start=(g == 0 and n == 0),
+                    stop=(g == PASSES - 1 and n == PACK - 1),
+                )
+
+        def multiply(a, t):
+            h_rounded[a, t] = stage.tile([P, PACK * CHUNK], BF16, name="h", tag="h", bufs=4, align_bytes=64)
+            nc.vector.tensor_tensor(
+                out=h_rounded[a, t][:].rearrange("p (c i j) -> p c j i", i=2, j=PACK),
+                in0=px[a, t][:].rearrange("p (j c i) -> p c j i", i=2, j=PACK),
+                in1=pc[a][:, :, t * CHUNK : (t + 1) * CHUNK].rearrange("p j (c i) -> p c j i", i=2),
+                op=mybir.AluOpType.mult,
+            )
+
+        def quantize_h(a, t):
+            h_q[a, t] = operand("h%d%d" % (a, t), CHUNK)
+            quantize(h_q[a, t], 0, h_rounded[a, t], E4M3)
+
+        def project(t, a, b, n0, width):
+            if a == 0:
+                y[t, n0] = bank(b)
+            step = M if width == M else P
+            for n in range(n0, n0 + width, step):
+                nc.tensor.matmul_mx(
+                    out=y[t, n0][:, n - n0 : n - n0 + step],
+                    lhsT=h_q[a, t][0][:].bitcast(E4M3),
+                    lhsT_scale=h_q[a, t][1][:],
+                    rhs=w_codes[:, a, 2 * n : 2 * (n + step)].bitcast(E2M1),
+                    rhs_scale=w_plane[:, a, n : n + step],
+                    start=(a == 0 and n == n0),
+                    stop=(a == GROUPS - 1 and n + step == n0 + width),
+                )
+
+        def store(t):
+            result = keep.tile([P, M], F32, name="result%d" % t)
+            nc.scalar.copy(out=result[:], in_=y[t, 0][:])
+            nc.sync.dma_start(out=out[t * CHUNK : (t + 1) * CHUNK, :], in_=result[:])
+
+        save_pc(0)
+        save_pc(1)
+        x01 = [round_stream("vector", x01_raw[g], 0, 2 * CHUNK) for g in range(PASSES)]
+        for g in range(PASSES):
+            quantize_x(g, 0, x01[g])
+        for g in range(PASSES):
+            prepare_wx(0, g, ("vector" if g == 0 else "scalar", "vector"))
+            px_pass(0, 0, g)
+            px_pass(0, 1, g)
+
+        def quantize_wx(g, u, rounded, m0=0):
+            if (1, g, u) not in wx_q:
+                wx_q[1, g, u] = operand("wx1%d%d" % (g, u), UNIT)
+            if rounded.shape[1] == PACK * UNIT:
+                quantize(wx_q[1, g, u], 0, rounded, E4M3)
+            else:
+                for i in range(2):
+                    quantize(wx_q[1, g, u], i * P + m0, rounded[:, i * UNIT : (i + 1) * UNIT], E4M3)
+
+        multiply(0, 0)
+        multiply(0, 1)
+        for g in range(2):
+            rounded = [round_weight(("scalar", "vector")[u], wx_raw[1, g], 0, u) for u in range(2)]
+            quantize_h(0, g)
+            for u in ((0, 1), (1, 0))[g]:
+                quantize_wx(g, u, rounded[u])
+            px_pass(1, 0, g)
+            px_pass(1, 1, g)
+        g = PASSES - 1
+        low = [round_weight(("scalar", "vector")[u], wx_last[0], 0, u, UNIT) for u in range(2)]
+        quantize_wx(g, 0, low[0], 0)
+        high = [round_weight(("scalar", "vector")[u], wx_last[1], 0, u, UNIT) for u in range(2)]
+        quantize_wx(g, 1, low[1], 0)
+        quantize_wx(g, 1, high[1], P // 2)
+        quantize_wx(g, 0, high[0], P // 2)
+        px_pass(1, 0, g)
+        px_pass(1, 1, g)
+
+        def prepare_x(g, t, tiles):
+            quantize_x(g, t, round_stream("scalar", tiles[g], 0, CHUNK))
+
+        def both(t, g):
+            for a in range(GROUPS):
+                px_pass(a, t, g)
+
+        prepare_x(0, 2, x2_raw)
+        both(2, 0)
+        multiply(1, 0)
+        prepare_x(1, 2, x2_raw)
+        both(2, 1)
+        multiply(1, 1)
+        prepare_x(2, 2, x2_raw)
+        both(2, 2)
+        quantize_h(1, 0)
+        quantize_h(1, 1)
+        for t in range(2):
+            for a in range(GROUPS):
+                project(t, a, t, 0, M)
+        multiply(0, 2)
+        prepare_x(0, 3, x3_raw)
+        both(3, 0)
+        prepare_x(1, 3, x3_raw)
+        px_pass(0, 3, 1)
+        multiply(1, 2)
+        prepare_x(2, 3, x3_raw)
+        px_pass(0, 3, 2)
+        px_pass(1, 3, 1)
+        px_pass(1, 3, 2)
+        quantize_h(0, 2)
+        quantize_h(1, 2)
+        for a in range(GROUPS):
+            project(2, a, 2, 0, M)
+        multiply(0, 3)
+        multiply(1, 3)
+        for t in range(3):
+            store(t)
+        half = M // 2
+        for a in range(GROUPS):
+            quantize_h(a, 3)
+            project(3, a, 3, 0, half)
+            project(3, a, 4, half, half)
+        result = keep.tile([P, M], F32, name="result3")
+        nc.scalar.copy(out=result[:, :half], in_=y[3, 0][:, :half])
+        nc.vector.tensor_copy(out=result[:, half:], in_=y[3, half][:, :half])
+        nc.sync.dma_start(out=out[3 * CHUNK :, :], in_=result[:])

@@ -21,7 +21,8 @@ PASSES = K // K_PASS
 GROUPS = R // K_PASS
 CHUNK = 128
 CHUNKS = T // CHUNK
-UNIT = 256
+HALF = 256
+SLOT_ORDER = (2, 3, 0, 1)
 
 
 def tile_mix_bilin_tm_none_kernel(tc, x, wx, c, wc, w_words, w_scales, out):
@@ -46,16 +47,16 @@ def tile_mix_bilin_tm_none_kernel(tc, x, wx, c, wc, w_words, w_scales, out):
             else:
                 nc.scalar.copy(out=dst, in_=src)
 
-        def round_stream(engine, tile, col0, width):
-            rounded = stage.tile([P, PACK * width], BF16, name="rounded", tag="rounded", align_bytes=64)
+        def round_stream(engine, tile, col0):
+            rounded = stage.tile([P, PACK * HALF], BF16, name="rounded", tag="rounded", align_bytes=64)
             copy(
                 engine,
                 rounded[:].rearrange("p (c i j) -> p c j i", i=2, j=PACK),
-                tile[:, :, col0 : col0 + width].rearrange("p j (c i) -> p c j i", i=2),
+                tile[:, :, col0 : col0 + HALF].rearrange("p j (c i) -> p c j i", i=2),
             )
             return rounded
 
-        def round_weight(engine, tile, col0, u, width=K_PASS):
+        def round_weight(engine, tile, col0, width, u):
             rounded = stage.tile([P, 2 * width], BF16, name="rounded", tag="rounded", align_bytes=64)
             src = tile[:, :, col0 : col0 + width].rearrange("p j (m u i) -> p u m j i", u=2, i=2)
             copy(engine, rounded[:].rearrange("p (i m j) -> p m j i", i=2, j=PACK), src[:, u])
@@ -71,14 +72,14 @@ def tile_mix_bilin_tm_none_kernel(tc, x, wx, c, wc, w_words, w_scales, out):
             nc.vector.quantize_mx(
                 out=dst[0][:, col0 : col0 + width].bitcast(fmt),
                 scales=dst[1][:, col0 : col0 + width],
-                in_=rounded,
+                in_=rounded[:],
             )
 
         def bank(b):
             return psum.tile([P, 512], F32, name="bank%d" % b, tag="bank%d" % b)
 
         c_raw = [load(c, 0, 0, T, "wide", 6)]
-        wc_raw = [load(wc, 0, 0, R, "wc", PASSES)]
+        wc_raw = [load(wc, 0, 0, R, "full", PASSES)]
         w_plane = keep.tile([P, GROUPS, M], U8, name="w_plane", align_bytes=64)
         nc.vector.memset(w_plane[:].bitcast(I32), 0)
         for q in range(4):
@@ -88,26 +89,23 @@ def tile_mix_bilin_tm_none_kernel(tc, x, wx, c, wc, w_words, w_scales, out):
             )
         for g in range(1, PASSES):
             c_raw.append(load(c, g, 0, T, "wide", 6))
-            wc_raw.append(load(wc, g, 0, R, "wc", PASSES))
-        x01_raw = [load(x, g, 0, 2 * CHUNK, "x01", PASSES) for g in range(PASSES)]
-        wx_raw = {}
-        for g in range(PASSES):
-            wx_raw[0, g] = load(wx, g, 0, K_PASS, "wide", 6)
+            wc_raw.append(load(wc, g, 0, R, "full", PASSES))
+        x_raw = [load(x, g, 0, T, "wide", 6) for g in range(PASSES)]
 
         pc_banks = [bank(b) for b in range(GROUPS * PACK)]
         for g in range(PASSES):
             c_q = operand("c%d" % g, T)
-            first = round_stream("scalar", c_raw[g], 0, UNIT)
-            second = round_stream("vector", c_raw[g], UNIT, UNIT)
-            quantize(c_q, UNIT, second, E5M2)
+            first = round_stream("scalar", c_raw[g], 0)
+            second = round_stream("vector", c_raw[g], HALF)
+            quantize(c_q, HALF, second, E5M2)
             quantize(c_q, 0, first, E5M2)
             rounded = {}
             for a in range(GROUPS):
-                rounded[a, 0] = round_weight("scalar", wc_raw[g], a * K_PASS, 0)
-                rounded[a, 1] = round_weight("vector", wc_raw[g], a * K_PASS, 1)
+                rounded[a, 0] = round_weight("scalar", wc_raw[g], a * K_PASS, K_PASS, 0)
+                rounded[a, 1] = round_weight("vector", wc_raw[g], a * K_PASS, K_PASS, 1)
             for a in range(GROUPS):
                 for u in (1, 0):
-                    wc_q = operand("wc%d%d%d" % (g, a, u), UNIT)
+                    wc_q = operand("wc%d%d%d" % (g, a, u), HALF)
                     quantize(wc_q, 0, rounded[a, u], E4M3)
                     for i in range(2):
                         cols = slice(i * P, (i + 1) * P)
@@ -121,51 +119,54 @@ def tile_mix_bilin_tm_none_kernel(tc, x, wx, c, wc, w_words, w_scales, out):
                             stop=(g == PASSES - 1),
                         )
 
-        for g in range(PASSES - 1):
-            wx_raw[1, g] = load(wx, g, K_PASS, K_PASS, "wide", 6)
-        wx_last = [load(wx, PASSES - 1, K_PASS + n * UNIT, UNIT, "wx_last", 2) for n in range(2)]
-        x2_raw = [load(x, g, 2 * CHUNK, CHUNK, "x2", PASSES) for g in range(PASSES)]
+        wx_raw = {(0, g): load(wx, g, 0, K_PASS, "wide", 6) for g in range(PASSES)}
+        wx_raw.update({(1, g): load(wx, g, K_PASS, K_PASS, "late", 2) for g in range(PASSES - 1)})
+        wx_last = [load(wx, PASSES - 1, K_PASS + n * HALF, HALF, "last", 2) for n in range(2)]
         w_codes = keep.tile([P, GROUPS, 2 * M], U8, name="w_codes", align_bytes=64)
         nc.sync.dma_start(out=w_codes[:].bitcast(I32), in_=w_words.rearrange("a p n -> p a n").bitcast(I32))
-        x3_raw = [load(x, g, 3 * CHUNK, CHUNK, "x3", PASSES) for g in range(PASSES)]
 
         pc = [keep.tile([P, PACK, T], F32, name="pc%d" % a) for a in range(GROUPS)]
-
-        def save_pc(a):
-            for j in (2, 3, 0, 1):
+        for a in range(GROUPS):
+            for j in SLOT_ORDER:
                 nc.scalar.copy(out=pc[a][:, j, :], in_=pc_banks[a * PACK + j][:])
 
-        wx_q, x_q, px, h_rounded, h_q, y = {}, {}, {}, {}, {}, {}
+        x_q = [operand("x%d" % g, T) for g in range(PASSES)]
+        for g in range(PASSES):
+            rounded = [round_stream("vector", x_raw[g], n * HALF) for n in range(2)]
+            for n in range(2):
+                quantize(x_q[g], n * HALF, rounded[n], E4M3)
 
-        def prepare_wx(a, g, engines):
-            rounded = [round_weight(engines[u], wx_raw[a, g], 0, u) for u in range(2)]
-            for u in (1, 0):
-                wx_q[a, g, u] = operand("wx%d%d%d" % (a, g, u), UNIT)
-                quantize(wx_q[a, g, u], 0, rounded[u], E4M3)
+        wx_q = {(a, g, u): operand("wx%d%d%d" % (a, g, u), HALF) for a in range(GROUPS) for g in range(PASSES) for u in range(2)}
+        px, h_rounded, h_q, y = {}, {}, {}, {}
 
-        def quantize_x(g, t, rounded):
-            chunks = rounded.shape[1] // (PACK * CHUNK)
-            dst = operand("x%d%d" % (g, t), chunks * CHUNK)
-            quantize(dst, 0, rounded, E4M3)
-            for n in range(chunks):
-                cols = slice(n * CHUNK, (n + 1) * CHUNK)
-                x_q[g, t + n] = (dst[0][:, cols], dst[1][:, cols])
+        started = set()
 
-        def px_pass(a, t, g):
-            if g == 0:
-                px[a, t] = bank(2 * (t // 2) * 2 + (2 * a + t if t < 2 else 2 * (t - 2) + a))
-            for n, j in enumerate((2, 3, 0, 1)):
+        def px_slots(a, g, t, slots):
+            first = (a, t) not in px
+            if first:
+                px[a, t] = bank(a * CHUNKS + t)
+            rows = slice(t * CHUNK, (t + 1) * CHUNK)
+            for j in slots:
                 codes, scales = wx_q[a, g, j // 2]
                 cols = slice((j % 2) * P, (j % 2 + 1) * P)
+                started.add((a, g, t, j))
                 nc.tensor.matmul_mx(
                     out=px[a, t][:, j * CHUNK : (j + 1) * CHUNK],
                     lhsT=codes[:, cols].bitcast(E4M3),
                     lhsT_scale=scales[:, cols],
-                    rhs=x_q[g, t][0].bitcast(E4M3),
-                    rhs_scale=x_q[g, t][1],
-                    start=(g == 0 and n == 0),
-                    stop=(g == PASSES - 1 and n == PACK - 1),
+                    rhs=x_q[g][0][:, rows].bitcast(E4M3),
+                    rhs_scale=x_q[g][1][:, rows],
+                    start=(first and j == slots[0]),
+                    stop=all((a, n, t, i) in started for n in range(PASSES) for i in range(PACK)),
                 )
+
+        def px_unit(a, g, u):
+            for t in range(CHUNKS):
+                px_slots(a, g, t, (2 * u, 2 * u + 1))
+
+        def px_pass(a, g):
+            for t in range(CHUNKS):
+                px_slots(a, g, t, SLOT_ORDER)
 
         def multiply(a, t):
             h_rounded[a, t] = stage.tile([P, PACK * CHUNK], BF16, name="h", tag="h", bufs=4, align_bytes=64)
@@ -180,7 +181,7 @@ def tile_mix_bilin_tm_none_kernel(tc, x, wx, c, wc, w_words, w_scales, out):
             h_q[a, t] = operand("h%d%d" % (a, t), CHUNK)
             quantize(h_q[a, t], 0, h_rounded[a, t], E4M3)
 
-        def project(t, a, b, n0, width):
+        def project(a, t, b, n0, width):
             if a == 0:
                 y[t, n0] = bank(b)
             step = M if width == M else P
@@ -195,93 +196,68 @@ def tile_mix_bilin_tm_none_kernel(tc, x, wx, c, wc, w_words, w_scales, out):
                     stop=(a == GROUPS - 1 and n + step == n0 + width),
                 )
 
-        def store(t):
+        def round_wx(a, g, engines):
+            return [round_weight(engines[u], wx_raw[a, g], 0, K_PASS, u) for u in range(2)]
+
+        def quantize_wx(a, g, u, rounded):
+            quantize(wx_q[a, g, u], 0, rounded[u], E4M3)
+            px_unit(a, g, u)
+
+        for g in range(PASSES):
+            rounded = round_wx(0, g, ("scalar", "vector"))
+            for u in (1, 0):
+                quantize_wx(0, g, u, rounded)
+        rounded = round_wx(1, 0, ("scalar", "scalar"))
+        multiply(0, 0)
+        multiply(0, 1)
+        quantize_h(0, 0)
+        multiply(0, 2)
+        quantize_wx(1, 0, 0, rounded)
+        multiply(0, 3)
+        quantize_wx(1, 0, 1, rounded)
+        rounded = round_wx(1, 1, ("scalar", "vector"))
+        quantize_h(0, 1)
+        quantize_h(0, 2)
+        for u in (1, 0):
+            quantize_wx(1, 1, u, rounded)
+
+        def quantize_last(u, n, rounded):
+            for i in range(2):
+                quantize(wx_q[1, PASSES - 1, u], i * P + n * (P // 2), rounded[:, i * HALF : (i + 1) * HALF], E4M3)
+
+        low = [round_weight(("scalar", "vector")[u], wx_last[0], 0, HALF, u) for u in range(2)]
+        quantize_last(0, 0, low[0])
+        quantize_h(0, 3)
+        high = [round_weight(("scalar", "vector")[u], wx_last[1], 0, HALF, u) for u in range(2)]
+        quantize_last(1, 0, low[1])
+        quantize_last(1, 1, high[1])
+        quantize_last(0, 1, high[0])
+        px_pass(1, PASSES - 1)
+
+        def finish(t):
+            quantize_h(1, t)
+            project(1, t, t, 0, M)
             result = keep.tile([P, M], F32, name="result%d" % t)
             nc.scalar.copy(out=result[:], in_=y[t, 0][:])
             nc.sync.dma_start(out=out[t * CHUNK : (t + 1) * CHUNK, :], in_=result[:])
 
-        save_pc(0)
-        save_pc(1)
-        x01 = [round_stream("vector", x01_raw[g], 0, 2 * CHUNK) for g in range(PASSES)]
-        for g in range(PASSES):
-            quantize_x(g, 0, x01[g])
-        for g in range(PASSES):
-            prepare_wx(0, g, ("vector" if g == 0 else "scalar", "vector"))
-            px_pass(0, 0, g)
-            px_pass(0, 1, g)
-
-        def quantize_wx(g, u, rounded, m0=0):
-            if (1, g, u) not in wx_q:
-                wx_q[1, g, u] = operand("wx1%d%d" % (g, u), UNIT)
-            if rounded.shape[1] == PACK * UNIT:
-                quantize(wx_q[1, g, u], 0, rounded, E4M3)
-            else:
-                for i in range(2):
-                    quantize(wx_q[1, g, u], i * P + m0, rounded[:, i * UNIT : (i + 1) * UNIT], E4M3)
-
-        multiply(0, 0)
-        multiply(0, 1)
-        for g in range(2):
-            rounded = [round_weight(("scalar", "vector")[u], wx_raw[1, g], 0, u) for u in range(2)]
-            quantize_h(0, g)
-            for u in ((0, 1), (1, 0))[g]:
-                quantize_wx(g, u, rounded[u])
-            px_pass(1, 0, g)
-            px_pass(1, 1, g)
-        g = PASSES - 1
-        low = [round_weight(("scalar", "vector")[u], wx_last[0], 0, u, UNIT) for u in range(2)]
-        quantize_wx(g, 0, low[0], 0)
-        high = [round_weight(("scalar", "vector")[u], wx_last[1], 0, u, UNIT) for u in range(2)]
-        quantize_wx(g, 1, low[1], 0)
-        quantize_wx(g, 1, high[1], P // 2)
-        quantize_wx(g, 0, high[0], P // 2)
-        px_pass(1, 0, g)
-        px_pass(1, 1, g)
-
-        def prepare_x(g, t, tiles):
-            quantize_x(g, t, round_stream("scalar", tiles[g], 0, CHUNK))
-
-        def both(t, g):
-            for a in range(GROUPS):
-                px_pass(a, t, g)
-
-        prepare_x(0, 2, x2_raw)
-        both(2, 0)
+        last = CHUNKS - 1
         multiply(1, 0)
-        prepare_x(1, 2, x2_raw)
-        both(2, 1)
+        project(0, 0, 0, 0, M)
         multiply(1, 1)
-        prepare_x(2, 2, x2_raw)
-        both(2, 2)
-        quantize_h(1, 0)
-        quantize_h(1, 1)
-        for t in range(2):
-            for a in range(GROUPS):
-                project(t, a, t, 0, M)
-        multiply(0, 2)
-        prepare_x(0, 3, x3_raw)
-        both(3, 0)
-        prepare_x(1, 3, x3_raw)
-        px_pass(0, 3, 1)
+        project(0, 1, 1, 0, M)
+        finish(0)
         multiply(1, 2)
-        prepare_x(2, 3, x3_raw)
-        px_pass(0, 3, 2)
-        px_pass(1, 3, 1)
-        px_pass(1, 3, 2)
-        quantize_h(0, 2)
-        quantize_h(1, 2)
-        for a in range(GROUPS):
-            project(2, a, 2, 0, M)
-        multiply(0, 3)
-        multiply(1, 3)
-        for t in range(3):
-            store(t)
-        half = M // 2
-        for a in range(GROUPS):
-            quantize_h(a, 3)
-            project(3, a, 3, 0, half)
-            project(3, a, 4, half, half)
-        result = keep.tile([P, M], F32, name="result3")
-        nc.scalar.copy(out=result[:, :half], in_=y[3, 0][:, :half])
-        nc.vector.tensor_copy(out=result[:, half:], in_=y[3, half][:, :half])
-        nc.sync.dma_start(out=out[3 * CHUNK :, :], in_=result[:])
+        project(0, 2, 2, 0, M)
+        finish(1)
+        finish(2)
+        multiply(1, last)
+        project(0, last, last, 0, HALF)
+        project(0, last, CHUNKS, HALF, HALF)
+        quantize_h(1, last)
+        project(1, last, last, 0, HALF)
+        project(1, last, CHUNKS, HALF, HALF)
+        result = keep.tile([P, M], F32, name="result%d" % last)
+        nc.vector.tensor_copy(out=result[:, :HALF], in_=y[last, 0][:, :HALF])
+        nc.scalar.copy(out=result[:, HALF:], in_=y[last, HALF][:, :HALF])
+        nc.sync.dma_start(out=out[last * CHUNK :, :], in_=result[:])

@@ -47,12 +47,12 @@ def tile_mix_bilin_tm_none_kernel(tc, x, wx, c, wc, w_words, w_scales, out):
             else:
                 nc.scalar.copy(out=dst, in_=src)
 
-        def round_stream(engine, tile, col0):
-            rounded = stage.tile([P, PACK * HALF], BF16, name="rounded", tag="rounded", align_bytes=64)
+        def round_stream(engine, tile, col0, width):
+            rounded = stage.tile([P, PACK * width], BF16, name="rounded", tag="rounded", align_bytes=64)
             copy(
                 engine,
                 rounded[:].rearrange("p (c i j) -> p c j i", i=2, j=PACK),
-                tile[:, :, col0 : col0 + HALF].rearrange("p j (c i) -> p c j i", i=2),
+                tile[:, :, col0 : col0 + width].rearrange("p j (c i) -> p c j i", i=2),
             )
             return rounded
 
@@ -78,7 +78,11 @@ def tile_mix_bilin_tm_none_kernel(tc, x, wx, c, wc, w_words, w_scales, out):
         def bank(b):
             return psum.tile([P, 512], F32, name="bank%d" % b, tag="bank%d" % b)
 
-        c_raw = [load(c, 0, 0, T, "wide", 6)]
+        c_raw = raw.tile([P, PASSES, PACK, T], F32, name="c_raw")
+        nc.sync.dma_start(
+            out=c_raw[:].rearrange("p g j w -> p g (j w)"),
+            in_=c.rearrange("(g p j) w -> p g (j w)", g=PASSES, j=PACK),
+        )
         wc_raw = [load(wc, 0, 0, R, "full", PASSES)]
         w_plane = keep.tile([P, GROUPS, M], U8, name="w_plane", align_bytes=64)
         nc.vector.memset(w_plane[:].bitcast(I32), 0)
@@ -88,85 +92,86 @@ def tile_mix_bilin_tm_none_kernel(tc, x, wx, c, wc, w_words, w_scales, out):
                 in_=w_scales[:, 4 * q : 4 * q + 4, :].rearrange("a r n -> r a n").bitcast(I32),
             )
         for g in range(1, PASSES):
-            c_raw.append(load(c, g, 0, T, "wide", 6))
             wc_raw.append(load(wc, g, 0, R, "full", PASSES))
-        x_raw = [load(x, g, 0, T, "wide", 6) for g in range(PASSES)]
+
+        c_q = [operand("c%d" % g, T) for g in range(PASSES)]
+        for g in range(PASSES):
+            first = round_stream("scalar", c_raw[:, g], 0, HALF)
+            second = round_stream("vector", c_raw[:, g], HALF, HALF)
+            if g > 0:
+                quantize(c_q[g - 1], 0, late, E5M2)
+            quantize(c_q[g], HALF, second, E5M2)
+            late = first
+        quantize(c_q[PASSES - 1], 0, late, E5M2)
+
+        def weight_pass(name, tile, g, use):
+            rounded = {}
+            for a in range(GROUPS):
+                rounded[a, 0] = round_weight("scalar", tile, a * K_PASS, K_PASS, 0)
+                rounded[a, 1] = round_weight("vector", tile, a * K_PASS, K_PASS, 1)
+            steps = []
+            for a in range(GROUPS):
+                for u in (1, 0):
+                    steps.append((a, u, rounded[a, u]))
+            return steps
 
         pc_banks = [bank(b) for b in range(GROUPS * PACK)]
         for g in range(PASSES):
-            c_q = operand("c%d" % g, T)
-            first = round_stream("scalar", c_raw[g], 0)
-            second = round_stream("vector", c_raw[g], HALF)
-            quantize(c_q, HALF, second, E5M2)
-            quantize(c_q, 0, first, E5M2)
-            rounded = {}
-            for a in range(GROUPS):
-                rounded[a, 0] = round_weight("scalar", wc_raw[g], a * K_PASS, K_PASS, 0)
-                rounded[a, 1] = round_weight("vector", wc_raw[g], a * K_PASS, K_PASS, 1)
-            for a in range(GROUPS):
-                for u in (1, 0):
-                    wc_q = operand("wc%d%d%d" % (g, a, u), HALF)
-                    quantize(wc_q, 0, rounded[a, u], E4M3)
-                    for i in range(2):
-                        cols = slice(i * P, (i + 1) * P)
-                        nc.tensor.matmul_mx(
-                            out=pc_banks[a * PACK + 2 * u + i][:],
-                            lhsT=wc_q[0][:, cols].bitcast(E4M3),
-                            lhsT_scale=wc_q[1][:, cols],
-                            rhs=c_q[0][:].bitcast(E5M2),
-                            rhs_scale=c_q[1][:],
-                            start=(g == 0),
-                            stop=(g == PASSES - 1),
-                        )
+            for a, u, rounded in weight_pass("wc", wc_raw[g], g, None):
+                wc_q = operand("wc%d%d%d" % (g, a, u), HALF)
+                quantize(wc_q, 0, rounded, E4M3)
+                for i in range(2):
+                    cols = slice(i * P, (i + 1) * P)
+                    nc.tensor.matmul_mx(
+                        out=pc_banks[a * PACK + 2 * u + i][:],
+                        lhsT=wc_q[0][:, cols].bitcast(E4M3),
+                        lhsT_scale=wc_q[1][:, cols],
+                        rhs=c_q[g][0][:].bitcast(E5M2),
+                        rhs_scale=c_q[g][1][:],
+                        start=(g == 0),
+                        stop=(g == PASSES - 1),
+                    )
 
-        wx_raw = {(0, g): load(wx, g, 0, K_PASS, "wide", 6) for g in range(PASSES)}
-        wx_raw.update({(1, g): load(wx, g, K_PASS, K_PASS, "late", 2) for g in range(PASSES - 1)})
-        wx_last = [load(wx, PASSES - 1, K_PASS + n * HALF, HALF, "last", 2) for n in range(2)]
+        wx_raw = [load(wx, g, 0, R, "full", PASSES) for g in range(PASSES)]
+        x_raw = {}
+        for n in range(2):
+            for g in range(PASSES):
+                x_raw[g, n] = load(x, g, n * HALF, HALF, "half", 6)
         w_codes = keep.tile([P, GROUPS, 2 * M], U8, name="w_codes", align_bytes=64)
         nc.sync.dma_start(out=w_codes[:].bitcast(I32), in_=w_words.rearrange("a p n -> p a n").bitcast(I32))
 
         pc = [keep.tile([P, PACK, T], F32, name="pc%d" % a) for a in range(GROUPS)]
         for a in range(GROUPS):
             for j in SLOT_ORDER:
-                nc.scalar.copy(out=pc[a][:, j, :], in_=pc_banks[a * PACK + j][:])
+                copy(("scalar", "vector")[a], pc[a][:, j, :], pc_banks[a * PACK + j][:])
 
-        x_q = [operand("x%d" % g, T) for g in range(PASSES)]
-        for g in range(PASSES):
-            rounded = [round_stream("vector", x_raw[g], n * HALF) for n in range(2)]
-            for n in range(2):
-                quantize(x_q[g], n * HALF, rounded[n], E4M3)
-
+        x_q = {(g, n): operand("x%d%d" % (g, n), HALF) for g in range(PASSES) for n in range(2)}
         wx_q = {(a, g, u): operand("wx%d%d%d" % (a, g, u), HALF) for a in range(GROUPS) for g in range(PASSES) for u in range(2)}
         px, h_rounded, h_q, y = {}, {}, {}, {}
-
-        started = set()
+        done = {}
 
         def px_slots(a, g, t, slots):
-            first = (a, t) not in px
-            if first:
-                px[a, t] = bank(a * CHUNKS + t)
-            rows = slice(t * CHUNK, (t + 1) * CHUNK)
+            if (a, t) not in px:
+                px[a, t] = bank(GROUPS * t + a)
+                done[a, t] = 0
+            n, col0 = divmod(t * CHUNK, HALF)
+            rows = slice(col0, col0 + CHUNK)
             for j in slots:
                 codes, scales = wx_q[a, g, j // 2]
                 cols = slice((j % 2) * P, (j % 2 + 1) * P)
-                started.add((a, g, t, j))
                 nc.tensor.matmul_mx(
                     out=px[a, t][:, j * CHUNK : (j + 1) * CHUNK],
                     lhsT=codes[:, cols].bitcast(E4M3),
                     lhsT_scale=scales[:, cols],
-                    rhs=x_q[g][0][:, rows].bitcast(E4M3),
-                    rhs_scale=x_q[g][1][:, rows],
-                    start=(first and j == slots[0]),
-                    stop=all((a, n, t, i) in started for n in range(PASSES) for i in range(PACK)),
+                    rhs=x_q[g, n][0][:, rows].bitcast(E4M3),
+                    rhs_scale=x_q[g, n][1][:, rows],
+                    start=(done[a, t] == 0),
+                    stop=(done[a, t] == PASSES * PACK - 1),
                 )
+                done[a, t] = done[a, t] + 1
 
-        def px_unit(a, g, u):
-            for t in range(CHUNKS):
-                px_slots(a, g, t, (2 * u, 2 * u + 1))
-
-        def px_pass(a, g):
-            for t in range(CHUNKS):
-                px_slots(a, g, t, SLOT_ORDER)
+        def px_bank(a, g, t):
+            px_slots(a, g, t, range(PACK))
 
         def multiply(a, t):
             h_rounded[a, t] = stage.tile([P, PACK * CHUNK], BF16, name="h", tag="h", bufs=4, align_bytes=64)
@@ -196,62 +201,104 @@ def tile_mix_bilin_tm_none_kernel(tc, x, wx, c, wc, w_words, w_scales, out):
                     stop=(a == GROUPS - 1 and n + step == n0 + width),
                 )
 
-        def round_wx(a, g, engines):
-            return [round_weight(engines[u], wx_raw[a, g], 0, K_PASS, u) for u in range(2)]
+        def round_x(engine, g, t):
+            n, col0 = divmod(t * CHUNK, HALF)
+            return round_stream(engine, x_raw[g, n], col0, CHUNK)
 
-        def quantize_wx(a, g, u, rounded):
-            quantize(wx_q[a, g, u], 0, rounded[u], E4M3)
-            px_unit(a, g, u)
-
-        for g in range(PASSES):
-            rounded = round_wx(0, g, ("scalar", "vector"))
-            for u in (1, 0):
-                quantize_wx(0, g, u, rounded)
-        rounded = round_wx(1, 0, ("scalar", "scalar"))
-        multiply(0, 0)
-        multiply(0, 1)
-        quantize_h(0, 0)
-        multiply(0, 2)
-        quantize_wx(1, 0, 0, rounded)
-        multiply(0, 3)
-        quantize_wx(1, 0, 1, rounded)
-        rounded = round_wx(1, 1, ("scalar", "vector"))
-        quantize_h(0, 1)
-        quantize_h(0, 2)
-        for u in (1, 0):
-            quantize_wx(1, 1, u, rounded)
-
-        def quantize_last(u, n, rounded):
-            for i in range(2):
-                quantize(wx_q[1, PASSES - 1, u], i * P + n * (P // 2), rounded[:, i * HALF : (i + 1) * HALF], E4M3)
-
-        low = [round_weight(("scalar", "vector")[u], wx_last[0], 0, HALF, u) for u in range(2)]
-        quantize_last(0, 0, low[0])
-        quantize_h(0, 3)
-        high = [round_weight(("scalar", "vector")[u], wx_last[1], 0, HALF, u) for u in range(2)]
-        quantize_last(1, 0, low[1])
-        quantize_last(1, 1, high[1])
-        quantize_last(0, 1, high[0])
-        px_pass(1, PASSES - 1)
+        def quantize_x(g, t, rounded):
+            n, col0 = divmod(t * CHUNK, HALF)
+            quantize(x_q[g, n], col0, rounded, E4M3)
 
         def finish(t):
-            quantize_h(1, t)
-            project(1, t, t, 0, M)
+            for a in range(GROUPS):
+                project(a, t, t, 0, M)
             result = keep.tile([P, M], F32, name="result%d" % t)
             nc.scalar.copy(out=result[:], in_=y[t, 0][:])
             nc.sync.dma_start(out=out[t * CHUNK : (t + 1) * CHUNK, :], in_=result[:])
 
-        last = CHUNKS - 1
+        for g in range(PASSES - 1):
+            for a, u, rounded in weight_pass("wx", wx_raw[g], g, None):
+                quantize(wx_q[a, g, u], 0, rounded, E4M3)
+
+        def round_last(engine, a, u):
+            return round_weight(engine, wx_raw[2], a * K_PASS, K_PASS, u)
+
+        def both(g, t):
+            for a in range(GROUPS):
+                px_bank(a, g, t)
+
+        def emit(t):
+            result = keep.tile([P, M], F32, name="result%d" % t)
+            nc.scalar.copy(out=result[:], in_=y[t, 0][:])
+            nc.sync.dma_start(out=out[t * CHUNK : (t + 1) * CHUNK, :], in_=result[:])
+
+        w00 = round_last("scalar", 0, 0)
+        w01 = round_last("vector", 0, 1)
+        w11 = round_last("vector", 1, 1)
+        quantize(wx_q[0, 2, 1], 0, w01, E4M3)
+        r01 = round_x("scalar", 0, 1)
+        r00 = round_x("vector", 0, 0)
+        quantize(wx_q[0, 2, 0], 0, w00, E4M3)
+        quantize_x(0, 0, r00)
+        both(0, 0)
+        quantize_x(0, 1, r01)
+        both(0, 1)
+        w10 = round_last("scalar", 1, 0)
+        quantize(wx_q[1, 2, 1], 0, w11, E4M3)
+        r10 = round_x("vector", 1, 0)
+        r11 = round_x("scalar", 1, 1)
+        quantize(wx_q[1, 2, 0], 0, w10, E4M3)
+        quantize_x(1, 0, r10)
+        both(1, 0)
+        quantize_x(1, 1, r11)
+        r20 = round_x("vector", 2, 0)
+        r21 = round_x("scalar", 2, 1)
+        quantize_x(2, 0, r20)
+        both(2, 0)
+        quantize_x(2, 1, r21)
+        for a in range(GROUPS):
+            px_bank(a, 1, 1)
+            px_bank(a, 2, 1)
+        r02 = round_x("vector", 0, 2)
+        r03 = round_x("scalar", 0, 3)
+        multiply(0, 0)
+        quantize_x(0, 2, r02)
+        both(0, 2)
+        quantize_x(0, 3, r03)
+        both(0, 3)
+        r12 = round_x("scalar", 1, 2)
+        r13 = round_x("scalar", 1, 3)
         multiply(1, 0)
-        project(0, 0, 0, 0, M)
-        multiply(1, 1)
-        project(0, 1, 1, 0, M)
+        quantize_h(0, 0)
+        multiply(0, 1)
+        quantize_x(1, 2, r12)
+        both(1, 2)
+        r22 = round_x("vector", 2, 2)
+        r23 = round_x("scalar", 2, 3)
+        quantize_x(1, 3, r13)
+        px_bank(0, 1, 3)
+        quantize_x(2, 2, r22)
+        both(2, 2)
+        px_bank(1, 1, 3)
+        quantize_h(1, 0)
         finish(0)
-        multiply(1, 2)
-        project(0, 2, 2, 0, M)
+        multiply(1, 1)
+        quantize_x(2, 3, r23)
+        both(2, 3)
+        quantize_h(0, 1)
+        quantize_h(1, 1)
         finish(1)
-        finish(2)
-        multiply(1, last)
+        multiply(0, 2)
+        multiply(1, 2)
+        quantize_h(0, 2)
+        project(0, 2, 2, 0, M)
+        multiply(0, 3)
+        quantize_h(1, 2)
+        project(1, 2, 2, 0, M)
+        emit(2)
+        multiply(1, 3)
+        last = CHUNKS - 1
+        quantize_h(0, last)
         project(0, last, last, 0, HALF)
         project(0, last, CHUNKS, HALF, HALF)
         quantize_h(1, last)

@@ -140,10 +140,15 @@ def tile_mix_bilin_tm_none_kernel(tc, x, wx, c, wc, w_words, w_scales, out):
         w_codes = keep.tile([P, GROUPS, 2 * M], U8, name="w_codes", align_bytes=64)
         nc.sync.dma_start(out=w_codes[:].bitcast(I32), in_=w_words.rearrange("a p n -> p a n").bitcast(I32))
 
-        pc = [keep.tile([P, PACK, T], F32, name="pc%d" % a) for a in range(GROUPS)]
+        pc_rows = [keep.tile([P, PACK, T], F32, name="pc_rows%d" % a) for a in range(GROUPS)]
         for a in range(GROUPS):
             for j in SLOT_ORDER:
-                copy(("scalar", "vector")[a], pc[a][:, j, :], pc_banks[a * PACK + j][:])
+                copy(("scalar", "vector")[a], pc_rows[a][:, j, :], pc_banks[a * PACK + j][:])
+        pc = {}
+
+        def interleave_pc(a, t):
+            pc[a, t] = keep.tile([P, CHUNK, PACK], F32, name="pc%d%d" % (a, t))
+            nc.scalar.copy(out=pc[a, t][:], in_=pc_rows[a][:, :, t * CHUNK : (t + 1) * CHUNK].rearrange("p j c -> p c j"))
 
         x_q = {(g, n): operand("x%d%d" % (g, n), HALF) for g in range(PASSES) for n in range(2)}
         wx_q = {(a, g, u): operand("wx%d%d%d" % (a, g, u), HALF) for a in range(GROUPS) for g in range(PASSES) for u in range(2)}
@@ -176,9 +181,9 @@ def tile_mix_bilin_tm_none_kernel(tc, x, wx, c, wc, w_words, w_scales, out):
         def multiply(a, t):
             h_rounded[a, t] = stage.tile([P, PACK * CHUNK], BF16, name="h", tag="h", bufs=4, align_bytes=64)
             nc.vector.tensor_tensor(
-                out=h_rounded[a, t][:].rearrange("p (c i j) -> p c j i", i=2, j=PACK),
-                in0=px[a, t][:].rearrange("p (j c i) -> p c j i", i=2, j=PACK),
-                in1=pc[a][:, :, t * CHUNK : (t + 1) * CHUNK].rearrange("p j (c i) -> p c j i", i=2),
+                out=h_rounded[a, t][:].rearrange("p (c j) -> p c j", j=PACK),
+                in0=px[a, t][:].rearrange("p (j c) -> p c j", j=PACK),
+                in1=pc[a, t][:],
                 op=mybir.AluOpType.mult,
             )
 
@@ -219,6 +224,8 @@ def tile_mix_bilin_tm_none_kernel(tc, x, wx, c, wc, w_words, w_scales, out):
         for g in range(PASSES - 1):
             for a, u, rounded in weight_pass("wx", wx_raw[g], g, None):
                 quantize(wx_q[a, g, u], 0, rounded, E4M3)
+            for a in range(GROUPS):
+                interleave_pc(a, g)
 
         def round_last(engine, a, u):
             return round_weight(engine, wx_raw[2], a * K_PASS, K_PASS, u)
@@ -235,32 +242,36 @@ def tile_mix_bilin_tm_none_kernel(tc, x, wx, c, wc, w_words, w_scales, out):
         w00 = round_last("scalar", 0, 0)
         w01 = round_last("vector", 0, 1)
         w11 = round_last("vector", 1, 1)
-        quantize(wx_q[0, 2, 1], 0, w01, E4M3)
         r01 = round_x("scalar", 0, 1)
         r00 = round_x("vector", 0, 0)
-        quantize(wx_q[0, 2, 0], 0, w00, E4M3)
+        quantize(wx_q[0, 2, 1], 0, w01, E4M3)
         quantize_x(0, 0, r00)
         both(0, 0)
+        quantize(wx_q[0, 2, 0], 0, w00, E4M3)
         quantize_x(0, 1, r01)
-        both(0, 1)
+        px_bank(0, 0, 1)
         w10 = round_last("scalar", 1, 0)
-        quantize(wx_q[1, 2, 1], 0, w11, E4M3)
         r10 = round_x("vector", 1, 0)
         r11 = round_x("scalar", 1, 1)
-        quantize(wx_q[1, 2, 0], 0, w10, E4M3)
+        quantize(wx_q[1, 2, 1], 0, w11, E4M3)
         quantize_x(1, 0, r10)
         both(1, 0)
-        quantize_x(1, 1, r11)
+        quantize(wx_q[1, 2, 0], 0, w10, E4M3)
         r20 = round_x("vector", 2, 0)
         r21 = round_x("scalar", 2, 1)
+        interleave_pc(0, 2)
+        quantize_x(1, 1, r11)
         quantize_x(2, 0, r20)
         both(2, 0)
         quantize_x(2, 1, r21)
-        for a in range(GROUPS):
-            px_bank(a, 1, 1)
-            px_bank(a, 2, 1)
+        px_bank(0, 1, 1)
+        px_bank(0, 2, 1)
+        px_bank(1, 0, 1)
+        px_bank(1, 1, 1)
+        px_bank(1, 2, 1)
         r02 = round_x("vector", 0, 2)
         r03 = round_x("scalar", 0, 3)
+        interleave_pc(1, 2)
         multiply(0, 0)
         quantize_x(0, 2, r02)
         both(0, 2)
@@ -275,6 +286,8 @@ def tile_mix_bilin_tm_none_kernel(tc, x, wx, c, wc, w_words, w_scales, out):
         both(1, 2)
         r22 = round_x("vector", 2, 2)
         r23 = round_x("scalar", 2, 3)
+        interleave_pc(0, 3)
+        interleave_pc(1, 3)
         quantize_x(1, 3, r13)
         px_bank(0, 1, 3)
         quantize_x(2, 2, r22)

@@ -147,8 +147,8 @@ def tile_mix_bilin_tm_none_kernel(tc, x, wx, c, wc, w_words, w_scales, out):
         pc = {}
 
         def interleave_pc(a, t):
-            pc[a, t] = keep.tile([P, CHUNK, PACK], F32, name="pc%d%d" % (a, t))
-            nc.scalar.copy(out=pc[a, t][:], in_=pc_rows[a][:, :, t * CHUNK : (t + 1) * CHUNK].rearrange("p j c -> p c j"))
+            pc[a, t] = keep.tile([P, CHUNK // 2, PACK, 2], F32, name="pc%d%d" % (a, t))
+            nc.scalar.copy(out=pc[a, t][:], in_=pc_rows[a][:, :, t * CHUNK : (t + 1) * CHUNK].rearrange("p j (c i) -> p c j i", i=2))
 
         x_q = {(g, n): operand("x%d%d" % (g, n), HALF) for g in range(PASSES) for n in range(2)}
         wx_q = {(a, g, u): operand("wx%d%d%d" % (a, g, u), HALF) for a in range(GROUPS) for g in range(PASSES) for u in range(2)}
@@ -181,8 +181,8 @@ def tile_mix_bilin_tm_none_kernel(tc, x, wx, c, wc, w_words, w_scales, out):
         def multiply(a, t):
             h_rounded[a, t] = stage.tile([P, PACK * CHUNK], BF16, name="h", tag="h", bufs=4, align_bytes=64)
             nc.vector.tensor_tensor(
-                out=h_rounded[a, t][:].rearrange("p (c j) -> p c j", j=PACK),
-                in0=px[a, t][:].rearrange("p (j c) -> p c j", j=PACK),
+                out=h_rounded[a, t][:].rearrange("p (c i j) -> p c j i", i=2, j=PACK),
+                in0=px[a, t][:].rearrange("p (j c i) -> p c j i", j=PACK, i=2),
                 in1=pc[a, t][:],
                 op=mybir.AluOpType.mult,
             )

@@ -22,6 +22,7 @@ GROUPS = R // K_PASS
 CHUNK = 128
 CHUNKS = T // CHUNK
 HALF = 256
+RUN = 4
 SLOT_ORDER = (2, 3, 0, 1)
 
 
@@ -86,11 +87,6 @@ def tile_mix_bilin_tm_none_kernel(tc, x, wx, c, wc, w_words, w_scales, out):
         wc_raw = [load(wc, 0, 0, R, "full", PASSES)]
         w_plane = keep.tile([P, GROUPS, M], U8, name="w_plane", align_bytes=64)
         nc.vector.memset(w_plane[:].bitcast(I32), 0)
-        for q in range(4):
-            nc.scalar.dma_start(
-                out=w_plane[32 * q : 32 * q + 4].bitcast(I32),
-                in_=w_scales[:, 4 * q : 4 * q + 4, :].rearrange("a r n -> r a n").bitcast(I32),
-            )
         for g in range(1, PASSES):
             wc_raw.append(load(wc, g, 0, R, "full", PASSES))
 
@@ -139,16 +135,16 @@ def tile_mix_bilin_tm_none_kernel(tc, x, wx, c, wc, w_words, w_scales, out):
                 x_raw[g, n] = load(x, g, n * HALF, HALF, "half", 6)
         w_codes = keep.tile([P, GROUPS, 2 * M], U8, name="w_codes", align_bytes=64)
         nc.sync.dma_start(out=w_codes[:].bitcast(I32), in_=w_words.rearrange("a p n -> p a n").bitcast(I32))
+        for q in range(4):
+            nc.sync.dma_start(
+                out=w_plane[32 * q : 32 * q + 4].bitcast(I32),
+                in_=w_scales[:, 4 * q : 4 * q + 4, :].rearrange("a r n -> r a n").bitcast(I32),
+            )
 
-        pc_rows = [keep.tile([P, PACK, T], F32, name="pc_rows%d" % a) for a in range(GROUPS)]
+        pc = [keep.tile([P, T // RUN, PACK, RUN], F32, name="pc%d" % a) for a in range(GROUPS)]
         for a in range(GROUPS):
             for j in SLOT_ORDER:
-                copy(("scalar", "vector")[a], pc_rows[a][:, j, :], pc_banks[a * PACK + j][:])
-        pc = {}
-
-        def interleave_pc(a, t):
-            pc[a, t] = keep.tile([P, CHUNK // 2, PACK, 2], F32, name="pc%d%d" % (a, t))
-            nc.scalar.copy(out=pc[a, t][:], in_=pc_rows[a][:, :, t * CHUNK : (t + 1) * CHUNK].rearrange("p j (c i) -> p c j i", i=2))
+                copy(("scalar", "vector")[a], pc[a][:, :, j, :], pc_banks[a * PACK + j][:].rearrange("p (c i) -> p c i", i=RUN))
 
         x_q = {(g, n): operand("x%d%d" % (g, n), HALF) for g in range(PASSES) for n in range(2)}
         wx_q = {(a, g, u): operand("wx%d%d%d" % (a, g, u), HALF) for a in range(GROUPS) for g in range(PASSES) for u in range(2)}
@@ -181,9 +177,9 @@ def tile_mix_bilin_tm_none_kernel(tc, x, wx, c, wc, w_words, w_scales, out):
         def multiply(a, t):
             h_rounded[a, t] = stage.tile([P, PACK * CHUNK], BF16, name="h", tag="h", bufs=4, align_bytes=64)
             nc.vector.tensor_tensor(
-                out=h_rounded[a, t][:].rearrange("p (c i j) -> p c j i", i=2, j=PACK),
-                in0=px[a, t][:].rearrange("p (j c i) -> p c j i", j=PACK, i=2),
-                in1=pc[a, t][:],
+                out=h_rounded[a, t][:].rearrange("p (c i j) -> p c j i", i=RUN, j=PACK),
+                in0=px[a, t][:].rearrange("p (j c i) -> p c j i", j=PACK, i=RUN),
+                in1=pc[a][:, t * CHUNK // RUN : (t + 1) * CHUNK // RUN],
                 op=mybir.AluOpType.mult,
             )
 
@@ -224,8 +220,6 @@ def tile_mix_bilin_tm_none_kernel(tc, x, wx, c, wc, w_words, w_scales, out):
         for g in range(PASSES - 1):
             for a, u, rounded in weight_pass("wx", wx_raw[g], g, None):
                 quantize(wx_q[a, g, u], 0, rounded, E4M3)
-            for a in range(GROUPS):
-                interleave_pc(a, g)
 
         def round_last(engine, a, u):
             return round_weight(engine, wx_raw[2], a * K_PASS, K_PASS, u)
@@ -259,7 +253,6 @@ def tile_mix_bilin_tm_none_kernel(tc, x, wx, c, wc, w_words, w_scales, out):
         quantize(wx_q[1, 2, 0], 0, w10, E4M3)
         r20 = round_x("vector", 2, 0)
         r21 = round_x("scalar", 2, 1)
-        interleave_pc(0, 2)
         quantize_x(1, 1, r11)
         quantize_x(2, 0, r20)
         both(2, 0)
@@ -271,7 +264,6 @@ def tile_mix_bilin_tm_none_kernel(tc, x, wx, c, wc, w_words, w_scales, out):
         px_bank(1, 2, 1)
         r02 = round_x("vector", 0, 2)
         r03 = round_x("scalar", 0, 3)
-        interleave_pc(1, 2)
         multiply(0, 0)
         quantize_x(0, 2, r02)
         both(0, 2)
@@ -286,8 +278,6 @@ def tile_mix_bilin_tm_none_kernel(tc, x, wx, c, wc, w_words, w_scales, out):
         both(1, 2)
         r22 = round_x("vector", 2, 2)
         r23 = round_x("scalar", 2, 3)
-        interleave_pc(0, 3)
-        interleave_pc(1, 3)
         quantize_x(1, 3, r13)
         px_bank(0, 1, 3)
         quantize_x(2, 2, r22)

@@ -48,8 +48,11 @@ def tile_mix_bilin_tm_none_kernel(tc, x, wx, c, wc, w_words, w_scales, out):
             else:
                 nc.scalar.copy(out=dst, in_=src)
 
+        def staged(width):
+            return stage.tile([P, width], BF16, name="rounded", tag="rounded", align_bytes=64)
+
         def round_stream(engine, tile, col0, width):
-            rounded = stage.tile([P, PACK * width], BF16, name="rounded", tag="rounded", align_bytes=64)
+            rounded = staged(PACK * width)
             copy(
                 engine,
                 rounded[:].rearrange("p (c i j) -> p c j i", i=2, j=PACK),
@@ -57,9 +60,9 @@ def tile_mix_bilin_tm_none_kernel(tc, x, wx, c, wc, w_words, w_scales, out):
             )
             return rounded
 
-        def round_weight(engine, tile, col0, width, u):
-            rounded = stage.tile([P, 2 * width], BF16, name="rounded", tag="rounded", align_bytes=64)
-            src = tile[:, :, col0 : col0 + width].rearrange("p j (m u i) -> p u m j i", u=2, i=2)
+        def round_weight(engine, tile, a, u):
+            rounded = staged(2 * K_PASS)
+            src = tile[:, :, a * K_PASS : (a + 1) * K_PASS].rearrange("p j (m u i) -> p u m j i", u=2, i=2)
             copy(engine, rounded[:].rearrange("p (i m j) -> p m j i", i=2, j=PACK), src[:, u])
             return rounded
 
@@ -84,8 +87,20 @@ def tile_mix_bilin_tm_none_kernel(tc, x, wx, c, wc, w_words, w_scales, out):
             out=c_raw[:].rearrange("p g j w -> p g (j w)"),
             in_=c.rearrange("(g p j) w -> p g (j w)", g=PASSES, j=PACK),
         )
-        wc_raw = [load(wc, 0, 0, R, "full", PASSES)]
         w_plane = keep.tile([P, GROUPS, M], U8, name="w_plane", align_bytes=64)
+        w_codes = keep.tile([P, GROUPS, 2 * M], U8, name="w_codes", align_bytes=64)
+
+        def load_scales(queue):
+            for q in range(4):
+                queue.dma_start(
+                    out=w_plane[32 * q : 32 * q + 4].bitcast(I32),
+                    in_=w_scales[:, 4 * q : 4 * q + 4, :].rearrange("a r n -> r a n").bitcast(I32),
+                )
+
+        def load_words():
+            nc.sync.dma_start(out=w_codes[:].bitcast(I32), in_=w_words.rearrange("a p n -> p a n").bitcast(I32))
+
+        wc_raw = [load(wc, 0, 0, R, "full", PASSES)]
         nc.vector.memset(w_plane[:].bitcast(I32), 0)
         for g in range(1, PASSES):
             wc_raw.append(load(wc, g, 0, R, "full", PASSES))
@@ -100,20 +115,16 @@ def tile_mix_bilin_tm_none_kernel(tc, x, wx, c, wc, w_words, w_scales, out):
             late = first
         quantize(c_q[PASSES - 1], 0, late, E5M2)
 
-        def weight_pass(name, tile, g, use):
+        def weight_pass(tile):
             rounded = {}
             for a in range(GROUPS):
-                rounded[a, 0] = round_weight("scalar", tile, a * K_PASS, K_PASS, 0)
-                rounded[a, 1] = round_weight("vector", tile, a * K_PASS, K_PASS, 1)
-            steps = []
-            for a in range(GROUPS):
-                for u in (1, 0):
-                    steps.append((a, u, rounded[a, u]))
-            return steps
+                rounded[a, 0] = round_weight("scalar", tile, a, 0)
+                rounded[a, 1] = round_weight("vector", tile, a, 1)
+            return [(a, u, rounded[a, u]) for a in range(GROUPS) for u in (1, 0)]
 
         pc_banks = [bank(b) for b in range(GROUPS * PACK)]
         for g in range(PASSES):
-            for a, u, rounded in weight_pass("wc", wc_raw[g], g, None):
+            for a, u, rounded in weight_pass(wc_raw[g]):
                 wc_q = operand("wc%d%d%d" % (g, a, u), HALF)
                 quantize(wc_q, 0, rounded, E4M3)
                 for i in range(2):
@@ -128,35 +139,26 @@ def tile_mix_bilin_tm_none_kernel(tc, x, wx, c, wc, w_words, w_scales, out):
                         stop=(g == PASSES - 1),
                     )
 
-        wx_raw = [load(wx, g, 0, R, "full", PASSES) for g in range(PASSES)]
-        x_raw = {}
-        for n in range(2):
-            for g in range(PASSES):
-                x_raw[g, n] = load(x, g, n * HALF, HALF, "half", 6)
-        w_codes = keep.tile([P, GROUPS, 2 * M], U8, name="w_codes", align_bytes=64)
-        nc.sync.dma_start(out=w_codes[:].bitcast(I32), in_=w_words.rearrange("a p n -> p a n").bitcast(I32))
-        for q in range(4):
-            nc.sync.dma_start(
-                out=w_plane[32 * q : 32 * q + 4].bitcast(I32),
-                in_=w_scales[:, 4 * q : 4 * q + 4, :].rearrange("a r n -> r a n").bitcast(I32),
-            )
-
         pc = [keep.tile([P, T // RUN, PACK, RUN], F32, name="pc%d" % a) for a in range(GROUPS)]
-        for a in range(GROUPS):
-            for j in SLOT_ORDER:
-                copy(("scalar", "vector")[a], pc[a][:, :, j, :], pc_banks[a * PACK + j][:].rearrange("p (c i) -> p c i", i=RUN))
 
-        x_q = {(g, n): operand("x%d%d" % (g, n), HALF) for g in range(PASSES) for n in range(2)}
+        def empty_pc(engine, a, j):
+            copy(engine, pc[a][:, :, j, :], pc_banks[a * PACK + j][:].rearrange("p (c i) -> p c i", i=RUN))
+
+        x_q = {(g, t): operand("x%d%d" % (g, t), CHUNK) for g in range(PASSES) for t in range(CHUNKS)}
         wx_q = {(a, g, u): operand("wx%d%d%d" % (a, g, u), HALF) for a in range(GROUPS) for g in range(PASSES) for u in range(2)}
         px, h_rounded, h_q, y = {}, {}, {}, {}
         done = {}
+        x_raw = {}
 
-        def px_slots(a, g, t, slots):
+        def load_x(g, t0, n):
+            tile = load(x, g, t0 * CHUNK, n * CHUNK, "x%d%d" % (g, t0), 1)
+            for t in range(t0, t0 + n):
+                x_raw[g, t] = (tile, (t - t0) * CHUNK)
+
+        def px_bank(a, g, t, slots=range(PACK)):
             if (a, t) not in px:
                 px[a, t] = bank(GROUPS * t + a)
                 done[a, t] = 0
-            n, col0 = divmod(t * CHUNK, HALF)
-            rows = slice(col0, col0 + CHUNK)
             for j in slots:
                 codes, scales = wx_q[a, g, j // 2]
                 cols = slice((j % 2) * P, (j % 2 + 1) * P)
@@ -164,22 +166,24 @@ def tile_mix_bilin_tm_none_kernel(tc, x, wx, c, wc, w_words, w_scales, out):
                     out=px[a, t][:, j * CHUNK : (j + 1) * CHUNK],
                     lhsT=codes[:, cols].bitcast(E4M3),
                     lhsT_scale=scales[:, cols],
-                    rhs=x_q[g, n][0][:, rows].bitcast(E4M3),
-                    rhs_scale=x_q[g, n][1][:, rows],
+                    rhs=x_q[g, t][0][:].bitcast(E4M3),
+                    rhs_scale=x_q[g, t][1][:],
                     start=(done[a, t] == 0),
                     stop=(done[a, t] == PASSES * PACK - 1),
                 )
                 done[a, t] = done[a, t] + 1
 
-        def px_bank(a, g, t):
-            px_slots(a, g, t, range(PACK))
+        def both(g, t):
+            for a in range(GROUPS):
+                px_bank(a, g, t)
 
         def multiply(a, t):
             h_rounded[a, t] = stage.tile([P, PACK * CHUNK], BF16, name="h", tag="h", bufs=4, align_bytes=64)
+            runs = slice(t * CHUNK // RUN, (t + 1) * CHUNK // RUN)
             nc.vector.tensor_tensor(
                 out=h_rounded[a, t][:].rearrange("p (c i j) -> p c j i", i=RUN, j=PACK),
                 in0=px[a, t][:].rearrange("p (j c i) -> p c j i", j=PACK, i=RUN),
-                in1=pc[a][:, t * CHUNK // RUN : (t + 1) * CHUNK // RUN],
+                in1=pc[a][:, runs],
                 op=mybir.AluOpType.mult,
             )
 
@@ -187,127 +191,134 @@ def tile_mix_bilin_tm_none_kernel(tc, x, wx, c, wc, w_words, w_scales, out):
             h_q[a, t] = operand("h%d%d" % (a, t), CHUNK)
             quantize(h_q[a, t], 0, h_rounded[a, t], E4M3)
 
-        def project(a, t, b, n0, width):
+        def project(a, t, b, n0=0, width=M):
             if a == 0:
                 y[t, n0] = bank(b)
-            step = M if width == M else P
-            for n in range(n0, n0 + width, step):
-                nc.tensor.matmul_mx(
-                    out=y[t, n0][:, n - n0 : n - n0 + step],
-                    lhsT=h_q[a, t][0][:].bitcast(E4M3),
-                    lhsT_scale=h_q[a, t][1][:],
-                    rhs=w_codes[:, a, 2 * n : 2 * (n + step)].bitcast(E2M1),
-                    rhs_scale=w_plane[:, a, n : n + step],
-                    start=(a == 0 and n == n0),
-                    stop=(a == GROUPS - 1 and n + step == n0 + width),
-                )
+            nc.tensor.matmul_mx(
+                out=y[t, n0][:, :width],
+                lhsT=h_q[a, t][0][:].bitcast(E4M3),
+                lhsT_scale=h_q[a, t][1][:],
+                rhs=w_codes[:, a, 2 * n0 : 2 * (n0 + width)].bitcast(E2M1),
+                rhs_scale=w_plane[:, a, n0 : n0 + width],
+                start=(a == 0),
+                stop=(a == GROUPS - 1),
+            )
 
         def round_x(engine, g, t):
-            n, col0 = divmod(t * CHUNK, HALF)
-            return round_stream(engine, x_raw[g, n], col0, CHUNK)
+            tile, col0 = x_raw[g, t]
+            return round_stream(engine, tile, col0, CHUNK)
+
+        def round_part(engine, g, t, rounded, col0, width):
+            tile, base = x_raw[g, t]
+            copy(
+                engine,
+                rounded[:, PACK * col0 : PACK * (col0 + width)].rearrange("p (c i j) -> p c j i", i=2, j=PACK),
+                tile[:, :, base + col0 : base + col0 + width].rearrange("p j (c i) -> p c j i", i=2),
+            )
 
         def quantize_x(g, t, rounded):
-            n, col0 = divmod(t * CHUNK, HALF)
-            quantize(x_q[g, n], col0, rounded, E4M3)
+            quantize(x_q[g, t], 0, rounded, E4M3)
 
-        def finish(t):
-            for a in range(GROUPS):
-                project(a, t, t, 0, M)
+        def emit(t, engine="scalar"):
             result = keep.tile([P, M], F32, name="result%d" % t)
-            nc.scalar.copy(out=result[:], in_=y[t, 0][:])
+            copy(engine, result[:], y[t, 0][:])
             nc.sync.dma_start(out=out[t * CHUNK : (t + 1) * CHUNK, :], in_=result[:])
 
+        def finish(t, b):
+            for a in range(GROUPS):
+                project(a, t, b)
+            emit(t)
+
+        def finish_last(b0, b1):
+            last = CHUNKS - 1
+            quantize_h(0, last)
+            project(0, last, b0, 0, HALF)
+            project(0, last, b1, HALF, HALF)
+            quantize_h(1, last)
+            project(1, last, b0, 0, HALF)
+            project(1, last, b1, HALF, HALF)
+            result = keep.tile([P, M], F32, name="result%d" % last)
+            nc.vector.tensor_copy(out=result[:, :HALF], in_=y[last, 0][:, :HALF])
+            nc.scalar.copy(out=result[:, HALF:], in_=y[last, HALF][:, :HALF])
+            nc.sync.dma_start(out=out[last * CHUNK :, :], in_=result[:])
+
+        wx_raw = [load(wx, g, 0, R, "full", PASSES) for g in range(PASSES)]
+        for n in range(2):
+            for g in range(PASSES):
+                load_x(g, 2 * n, 2)
+        load_words()
+        load_scales(nc.sync)
+        for j in SLOT_ORDER:
+            empty_pc("scalar", 0, j)
+        for j in SLOT_ORDER:
+            empty_pc("vector", 1, j)
         for g in range(PASSES - 1):
-            for a, u, rounded in weight_pass("wx", wx_raw[g], g, None):
+            for a, u, rounded in weight_pass(wx_raw[g]):
                 quantize(wx_q[a, g, u], 0, rounded, E4M3)
-
-        def round_last(engine, a, u):
-            return round_weight(engine, wx_raw[2], a * K_PASS, K_PASS, u)
-
-        def both(g, t):
-            for a in range(GROUPS):
-                px_bank(a, g, t)
-
-        def emit(t):
-            result = keep.tile([P, M], F32, name="result%d" % t)
-            nc.scalar.copy(out=result[:], in_=y[t, 0][:])
-            nc.sync.dma_start(out=out[t * CHUNK : (t + 1) * CHUNK, :], in_=result[:])
-
-        w00 = round_last("scalar", 0, 0)
-        w01 = round_last("vector", 0, 1)
-        w11 = round_last("vector", 1, 1)
-        r01 = round_x("scalar", 0, 1)
+        w00 = round_weight("scalar", wx_raw[2], 0, 0)
+        w01 = round_weight("vector", wx_raw[2], 0, 1)
+        w11 = round_weight("scalar", wx_raw[2], 1, 1)
+        w10 = round_weight("scalar", wx_raw[2], 1, 0)
         r00 = round_x("vector", 0, 0)
-        quantize(wx_q[0, 2, 1], 0, w01, E4M3)
+        r01 = round_x("vector", 0, 1)
         quantize_x(0, 0, r00)
         both(0, 0)
-        quantize(wx_q[0, 2, 0], 0, w00, E4M3)
+        quantize(wx_q[0, 2, 1], 0, w01, E4M3)
         quantize_x(0, 1, r01)
-        px_bank(0, 0, 1)
-        w10 = round_last("scalar", 1, 0)
+        both(0, 1)
         r10 = round_x("vector", 1, 0)
-        r11 = round_x("scalar", 1, 1)
-        quantize(wx_q[1, 2, 1], 0, w11, E4M3)
+        quantize(wx_q[0, 2, 0], 0, w00, E4M3)
         quantize_x(1, 0, r10)
         both(1, 0)
-        quantize(wx_q[1, 2, 0], 0, w10, E4M3)
+        quantize(wx_q[1, 2, 1], 0, w11, E4M3)
+        r11 = round_x("scalar", 1, 1)
         r20 = round_x("vector", 2, 0)
-        r21 = round_x("scalar", 2, 1)
-        quantize_x(1, 1, r11)
+        r21 = round_x("vector", 2, 1)
         quantize_x(2, 0, r20)
-        both(2, 0)
+        px_bank(0, 2, 0)
+        quantize(wx_q[1, 2, 0], 0, w10, E4M3)
+        px_bank(1, 2, 0)
         quantize_x(2, 1, r21)
-        px_bank(0, 1, 1)
-        px_bank(0, 2, 1)
-        px_bank(1, 0, 1)
-        px_bank(1, 1, 1)
-        px_bank(1, 2, 1)
-        r02 = round_x("vector", 0, 2)
+        quantize_x(1, 1, r11)
+        both(1, 1)
+        both(2, 1)
+        r02 = round_x("scalar", 0, 2)
         r03 = round_x("scalar", 0, 3)
+        r12 = round_x("scalar", 1, 2)
+        r13 = round_x("scalar", 1, 3)
         multiply(0, 0)
         quantize_x(0, 2, r02)
         both(0, 2)
+        multiply(1, 0)
         quantize_x(0, 3, r03)
         both(0, 3)
-        r12 = round_x("scalar", 1, 2)
-        r13 = round_x("scalar", 1, 3)
-        multiply(1, 0)
         quantize_h(0, 0)
         multiply(0, 1)
         quantize_x(1, 2, r12)
         both(1, 2)
-        r22 = round_x("vector", 2, 2)
+        r22 = staged(PACK * CHUNK)
+        round_part("vector", 2, 2, r22, 0, CHUNK // 2)
+        round_part("scalar", 2, 2, r22, CHUNK // 2, CHUNK // 2)
         r23 = round_x("scalar", 2, 3)
         quantize_x(1, 3, r13)
         px_bank(0, 1, 3)
+        quantize_h(1, 0)
         quantize_x(2, 2, r22)
         both(2, 2)
-        px_bank(1, 1, 3)
-        quantize_h(1, 0)
-        finish(0)
+        finish(0, 0)
         multiply(1, 1)
         quantize_x(2, 3, r23)
-        both(2, 3)
+        px_bank(0, 2, 3)
+        px_bank(1, 1, 3)
+        px_bank(1, 2, 3)
         quantize_h(0, 1)
         quantize_h(1, 1)
-        finish(1)
+        finish(1, 1)
         multiply(0, 2)
         multiply(1, 2)
         quantize_h(0, 2)
-        project(0, 2, 2, 0, M)
         multiply(0, 3)
         quantize_h(1, 2)
-        project(1, 2, 2, 0, M)
-        emit(2)
+        finish(2, 2)
         multiply(1, 3)
-        last = CHUNKS - 1
-        quantize_h(0, last)
-        project(0, last, last, 0, HALF)
-        project(0, last, CHUNKS, HALF, HALF)
-        quantize_h(1, last)
-        project(1, last, last, 0, HALF)
-        project(1, last, CHUNKS, HALF, HALF)
-        result = keep.tile([P, M], F32, name="result%d" % last)
-        nc.vector.tensor_copy(out=result[:, :HALF], in_=y[last, 0][:, :HALF])
-        nc.scalar.copy(out=result[:, HALF:], in_=y[last, HALF][:, :HALF])
-        nc.sync.dma_start(out=out[last * CHUNK :, :], in_=result[:])
+        finish_last(3, 4)

@@ -243,11 +243,7 @@ def tile_mix_bilin_tm_none_kernel(tc, x, wx, c, wc, w_words, w_scales, out):
             nc.sync.dma_start(out=out[last * CHUNK :, :], in_=result[:])
 
         wx_raw = [load(wx, g, 0, R, "full", PASSES) for g in range(PASSES)]
-        for n in range(2):
-            for g in range(PASSES):
-                load_x(g, 2 * n, 2)
-        load_words()
-        load_scales(nc.sync)
+        load_x(0, 0, 2)
         for j in SLOT_ORDER:
             empty_pc("scalar", 0, j)
         for j in SLOT_ORDER:
@@ -255,6 +251,18 @@ def tile_mix_bilin_tm_none_kernel(tc, x, wx, c, wc, w_words, w_scales, out):
         for g in range(PASSES - 1):
             for a, u, rounded in weight_pass(wx_raw[g]):
                 quantize(wx_q[a, g, u], 0, rounded, E4M3)
+        for g in (1, 2):
+            tile = raw.tile([P, PACK, HALF], F32, name="full", tag="full", bufs=PASSES)
+            rows = x[g * K_PASS : (g + 1) * K_PASS, :HALF].rearrange("(p j) w -> p j w", j=PACK)
+            slots = PACK if g == 1 else PACK // 2
+            nc.sync.dma_start(out=tile[:, :slots], in_=rows[:, :slots])
+            for t in range(2):
+                x_raw[g, t] = (tile, t * CHUNK)
+        nc.scalar.dma_start(out=tile[:, slots:], in_=rows[:, slots:])
+        for g in range(PASSES):
+            load_x(g, 2, 2)
+        load_words()
+        load_scales(nc.sync)
         w00 = round_weight("scalar", wx_raw[2], 0, 0)
         w01 = round_weight("vector", wx_raw[2], 0, 1)
         w11 = round_weight("scalar", wx_raw[2], 1, 1)

from contextlib import ExitStack

import concourse.mybir as mybir

K, L, R, M, T = 1536, 1536, 1024, 512, 512
FLOPS = 2 * (K * R * T + L * R * T + R * M * T)

F32 = mybir.dt.float32
BF16 = mybir.dt.bfloat16
U32 = mybir.dt.uint32
I32 = mybir.dt.int32
U8 = mybir.dt.uint8
E4M3 = mybir.dt.float8_e4m3fn_x4
E5M2 = mybir.dt.float8_e5m2_x4
E2M1 = mybir.dt.float4_e2m1fn_x4

P = 128
PACK = 4
K_PASS = P * PACK
PASSES = K // K_PASS
GROUPS = R // K_PASS
CHUNK = 128
CHUNKS = T // CHUNK
HALF = 256
RUN = 4
SLOT_ORDER = (2, 3, 0, 1)


def tile_mix_bilin_tm_none_kernel(tc, x, wx, c, wc, w_words, w_scales, out):
    nc = tc.nc

    with ExitStack() as ctx:
        raw = ctx.enter_context(tc.tile_pool(name="raw", bufs=1))
        stage = ctx.enter_context(tc.tile_pool(name="stage", bufs=8))
        keep = ctx.enter_context(tc.tile_pool(name="keep", bufs=1))
        psum = ctx.enter_context(tc.psum_pool(name="psum", bufs=1))
        ctx.enter_context(tc.manual_schedule())

        def load(src, g, col0, width, tag, bufs):
            tile = raw.tile([P, PACK, width], F32, name=tag, tag=tag, bufs=bufs)
            rows = src[g * K_PASS : (g + 1) * K_PASS, col0 : col0 + width]
            nc.sync.dma_start(out=tile[:], in_=rows.rearrange("(p j) w -> p j w", j=PACK))
            return tile

        def copy(engine, dst, src):
            if engine == "vector":
                nc.vector.tensor_copy(out=dst, in_=src)
            else:
                nc.scalar.copy(out=dst, in_=src)

        def staged(width):
            return stage.tile([P, width], BF16, name="rounded", tag="rounded", align_bytes=64)

        def round_stream(engine, tile, col0, width):
            rounded = staged(PACK * width)
            copy(
                engine,
                rounded[:].rearrange("p (c i j) -> p c j i", i=2, j=PACK),
                tile[:, :, col0 : col0 + width].rearrange("p j (c i) -> p c j i", i=2),
            )
            return rounded

        def round_weight(engine, tile, a, u):
            rounded = staged(2 * K_PASS)
            src = tile[:, :, a * K_PASS : (a + 1) * K_PASS].rearrange("p j (m u i) -> p u m j i", u=2, i=2)
            copy(engine, rounded[:].rearrange("p (i m j) -> p m j i", i=2, j=PACK), src[:, u])
            return rounded

        def operand(name, width):
            codes = keep.tile([P, width], U32, name=name + "_codes", align_bytes=64)
            scales = keep.tile([P, width], U8, name=name + "_scales", align_bytes=64)
            return codes, scales

        def quantize(dst, col0, rounded, fmt):
            width = rounded.shape[1] // PACK
            nc.vector.quantize_mx(
                out=dst[0][:, col0 : col0 + width].bitcast(fmt),
                scales=dst[1][:, col0 : col0 + width],
                in_=rounded[:],
            )

        def bank(b):
            return psum.tile([P, 512], F32, name="bank%d" % b, tag="bank%d" % b)

        c_raw = raw.tile([P, PASSES, PACK, T], F32, name="c_raw")
        nc.sync.dma_start(
            out=c_raw[:].rearrange("p g j w -> p g (j w)"),
            in_=c.rearrange("(g p j) w -> p g (j w)", g=PASSES, j=PACK),
        )
        w_plane = keep.tile([P, GROUPS, M], U8, name="w_plane", align_bytes=64)
        w_codes = keep.tile([P, GROUPS, 2 * M], U8, name="w_codes", align_bytes=64)

        def load_scales(queue):
            for q in range(4):
                queue.dma_start(
                    out=w_plane[32 * q : 32 * q + 4].bitcast(I32),
                    in_=w_scales[:, 4 * q : 4 * q + 4, :].rearrange("a r n -> r a n").bitcast(I32),
                )

        def load_words():
            nc.sync.dma_start(out=w_codes[:].bitcast(I32), in_=w_words.rearrange("a p n -> p a n").bitcast(I32))

        wc_raw = [load(wc, 0, 0, R, "full", PASSES)]
        nc.vector.memset(w_plane[:].bitcast(I32), 0)
        for g in range(1, PASSES):
            wc_raw.append(load(wc, g, 0, R, "full", PASSES))

        c_q = [operand("c%d" % g, T) for g in range(PASSES)]
        for g in range(PASSES):
            first = round_stream("scalar", c_raw[:, g], 0, HALF)
            second = round_stream("vector", c_raw[:, g], HALF, HALF)
            if g > 0:
                quantize(c_q[g - 1], 0, late, E5M2)
            quantize(c_q[g], HALF, second, E5M2)
            late = first
        quantize(c_q[PASSES - 1], 0, late, E5M2)

        def weight_pass(tile):
            rounded = {}
            for a in range(GROUPS):
                rounded[a, 0] = round_weight("scalar", tile, a, 0)
                rounded[a, 1] = round_weight("vector", tile, a, 1)
            return [(a, u, rounded[a, u]) for a in range(GROUPS) for u in (1, 0)]

        pc_banks = [bank(b) for b in range(GROUPS * PACK)]
        for g in range(PASSES):
            for a, u, rounded in weight_pass(wc_raw[g]):
                wc_q = operand("wc%d%d%d" % (g, a, u), HALF)
                quantize(wc_q, 0, rounded, E4M3)
                for i in range(2):
                    cols = slice(i * P, (i + 1) * P)
                    nc.tensor.matmul_mx(
                        out=pc_banks[a * PACK + 2 * u + i][:],
                        lhsT=wc_q[0][:, cols].bitcast(E4M3),
                        lhsT_scale=wc_q[1][:, cols],
                        rhs=c_q[g][0][:].bitcast(E5M2),
                        rhs_scale=c_q[g][1][:],
                        start=(g == 0),
                        stop=(g == PASSES - 1),
                    )

        pc = [keep.tile([P, T // RUN, PACK, RUN], F32, name="pc%d" % a) for a in range(GROUPS)]

        def empty_pc(engine, a, j):
            copy(engine, pc[a][:, :, j, :], pc_banks[a * PACK + j][:].rearrange("p (c i) -> p c i", i=RUN))

        x_q = {(g, t): operand("x%d%d" % (g, t), CHUNK) for g in range(PASSES) for t in range(CHUNKS)}
        wx_q = {(a, g, u): operand("wx%d%d%d" % (a, g, u), HALF) for a in range(GROUPS) for g in range(PASSES) for u in range(2)}
        px, h_rounded, h_q, y = {}, {}, {}, {}
        done = {}
        x_raw = {}

        def load_x(g, t0, n):
            tile = load(x, g, t0 * CHUNK, n * CHUNK, "x%d%d" % (g, t0), 1)
            for t in range(t0, t0 + n):
                x_raw[g, t] = (tile, (t - t0) * CHUNK)

        def px_bank(a, g, t, slots=range(PACK)):
            if (a, t) not in px:
                px[a, t] = bank(GROUPS * t + a)
                done[a, t] = 0
            for j in slots:
                codes, scales = wx_q[a, g, j // 2]
                cols = slice((j % 2) * P, (j % 2 + 1) * P)
                nc.tensor.matmul_mx(
                    out=px[a, t][:, j * CHUNK : (j + 1) * CHUNK],
                    lhsT=codes[:, cols].bitcast(E4M3),
                    lhsT_scale=scales[:, cols],
                    rhs=x_q[g, t][0][:].bitcast(E4M3),
                    rhs_scale=x_q[g, t][1][:],
                    start=(done[a, t] == 0),
                    stop=(done[a, t] == PASSES * PACK - 1),
                )
                done[a, t] = done[a, t] + 1

        def both(g, t):
            for a in range(GROUPS):
                px_bank(a, g, t)

        def multiply(a, t):
            h_rounded[a, t] = stage.tile([P, PACK * CHUNK], BF16, name="h", tag="h", bufs=4, align_bytes=64)
            runs = slice(t * CHUNK // RUN, (t + 1) * CHUNK // RUN)
            nc.vector.tensor_tensor(
                out=h_rounded[a, t][:].rearrange("p (c i j) -> p c j i", i=RUN, j=PACK),
                in0=px[a, t][:].rearrange("p (j c i) -> p c j i", j=PACK, i=RUN),
                in1=pc[a][:, runs],
                op=mybir.AluOpType.mult,
            )

        def quantize_h(a, t):
            h_q[a, t] = operand("h%d%d" % (a, t), CHUNK)
            quantize(h_q[a, t], 0, h_rounded[a, t], E4M3)

        def project(a, t, b, n0=0, width=M):
            if a == 0:
                y[t, n0] = bank(b)
            nc.tensor.matmul_mx(
                out=y[t, n0][:, :width],
                lhsT=h_q[a, t][0][:].bitcast(E4M3),
                lhsT_scale=h_q[a, t][1][:],
                rhs=w_codes[:, a, 2 * n0 : 2 * (n0 + width)].bitcast(E2M1),
                rhs_scale=w_plane[:, a, n0 : n0 + width],
                start=(a == 0),
                stop=(a == GROUPS - 1),
            )

        def round_x(engine, g, t):
            tile, col0 = x_raw[g, t]
            return round_stream(engine, tile, col0, CHUNK)

        def round_part(engine, g, t, rounded, col0, width):
            tile, base = x_raw[g, t]
            copy(
                engine,
                rounded[:, PACK * col0 : PACK * (col0 + width)].rearrange("p (c i j) -> p c j i", i=2, j=PACK),
                tile[:, :, base + col0 : base + col0 + width].rearrange("p j (c i) -> p c j i", i=2),
            )

        def quantize_x(g, t, rounded):
            quantize(x_q[g, t], 0, rounded, E4M3)

        def emit(t, engine="scalar"):
            result = keep.tile([P, M], F32, name="result%d" % t)
            copy(engine, result[:], y[t, 0][:])
            nc.sync.dma_start(out=out[t * CHUNK : (t + 1) * CHUNK, :], in_=result[:])

        def finish(t, b):
            for a in range(GROUPS):
                project(a, t, b)
            emit(t)

        def finish_last(b0, b1):
            last = CHUNKS - 1
            quantize_h(0, last)
            project(0, last, b0, 0, HALF)
            project(0, last, b1, HALF, HALF)
            quantize_h(1, last)
            project(1, last, b0, 0, HALF)
            project(1, last, b1, HALF, HALF)
            result = keep.tile([P, M], F32, name="result%d" % last)
            nc.vector.tensor_copy(out=result[:, :HALF], in_=y[last, 0][:, :HALF])
            nc.scalar.copy(out=result[:, HALF:], in_=y[last, HALF][:, :HALF])
            nc.sync.dma_start(out=out[last * CHUNK :, :], in_=result[:])

        wx_raw = [load(wx, g, 0, R, "full", PASSES) for g in range(PASSES)]
        load_x(0, 0, 2)
        for j in SLOT_ORDER:
            empty_pc("scalar", 0, j)
        for j in SLOT_ORDER:
            empty_pc("vector", 1, j)
        for g in range(PASSES - 1):
            for a, u, rounded in weight_pass(wx_raw[g]):
                quantize(wx_q[a, g, u], 0, rounded, E4M3)
        for g in (1, 2):
            tile = raw.tile([P, PACK, HALF], F32, name="full", tag="full", bufs=PASSES)
            rows = x[g * K_PASS : (g + 1) * K_PASS, :HALF].rearrange("(p j) w -> p j w", j=PACK)
            slots = PACK if g == 1 else PACK // 2
            nc.sync.dma_start(out=tile[:, :slots], in_=rows[:, :slots])
            for t in range(2):
                x_raw[g, t] = (tile, t * CHUNK)
        nc.scalar.dma_start(out=tile[:, slots:], in_=rows[:, slots:])
        for g in range(PASSES):
            load_x(g, 2, 2)
        load_words()
        load_scales(nc.sync)
        w00 = round_weight("scalar", wx_raw[2], 0, 0)
        w01 = round_weight("vector", wx_raw[2], 0, 1)
        w11 = round_weight("scalar", wx_raw[2], 1, 1)
        w10 = round_weight("scalar", wx_raw[2], 1, 0)
        r00 = round_x("vector", 0, 0)
        r01 = round_x("vector", 0, 1)
        quantize_x(0, 0, r00)
        both(0, 0)
        quantize(wx_q[0, 2, 1], 0, w01, E4M3)
        quantize_x(0, 1, r01)
        both(0, 1)
        r10 = round_x("vector", 1, 0)
        quantize(wx_q[0, 2, 0], 0, w00, E4M3)
        quantize_x(1, 0, r10)
        both(1, 0)
        quantize(wx_q[1, 2, 1], 0, w11, E4M3)
        r11 = round_x("scalar", 1, 1)
        r20 = round_x("vector", 2, 0)
        r21 = round_x("vector", 2, 1)
        quantize_x(2, 0, r20)
        px_bank(0, 2, 0)
        quantize(wx_q[1, 2, 0], 0, w10, E4M3)
        px_bank(1, 2, 0)
        quantize_x(2, 1, r21)
        quantize_x(1, 1, r11)
        both(1, 1)
        both(2, 1)
        r02 = round_x("scalar", 0, 2)
        r03 = round_x("scalar", 0, 3)
        r12 = round_x("scalar", 1, 2)
        r13 = round_x("scalar", 1, 3)
        multiply(0, 0)
        quantize_x(0, 2, r02)
        both(0, 2)
        multiply(1, 0)
        quantize_x(0, 3, r03)
        both(0, 3)
        quantize_h(0, 0)
        multiply(0, 1)
        quantize_x(1, 2, r12)
        both(1, 2)
        r22 = staged(PACK * CHUNK)
        round_part("vector", 2, 2, r22, 0, CHUNK // 2)
        round_part("scalar", 2, 2, r22, CHUNK // 2, CHUNK // 2)
        r23 = round_x("scalar", 2, 3)
        quantize_x(1, 3, r13)
        px_bank(0, 1, 3)
        quantize_h(1, 0)
        quantize_x(2, 2, r22)
        both(2, 2)
        finish(0, 0)
        multiply(1, 1)
        quantize_x(2, 3, r23)
        px_bank(0, 2, 3)
        px_bank(1, 1, 3)
        px_bank(1, 2, 3)
        quantize_h(0, 1)
        quantize_h(1, 1)
        finish(1, 1)
        multiply(0, 2)
        multiply(1, 2)
        quantize_h(0, 2)
        multiply(0, 3)
        quantize_h(1, 2)
        finish(2, 2)
        multiply(1, 3)
        finish_last(3, 4)
